import numpy as np
import ml_dtypes


def mxq(x, axis, fmt="e4m3"):
    dtype, down = {"e4m3": (ml_dtypes.float8_e4m3fn, 7), "e5m2": (ml_dtypes.float8_e5m2, 14)}[fmt]
    v = np.moveaxis(np.asarray(x, np.float32).astype(ml_dtypes.bfloat16).astype(np.float64), axis, -1)
    blocks = v.reshape(v.shape[:-1] + (-1, 32))
    amax = np.abs(blocks).max(-1, keepdims=True)
    byte = np.maximum(np.where(amax > 0, np.frexp(amax)[1] - 1 + 127, 0) - down, 1)
    scale = np.exp2(byte - 127.0)
    codes = (blocks / scale).astype(np.float32).astype(dtype).astype(np.float64)
    return np.moveaxis((codes * scale).reshape(v.shape), -1, axis)


WIDE = False


def mx_kscale(k):
    if not WIDE:
        return np.ones(k)
    levels = np.array([10, -10, 5, -5, 0])
    if k % 512:
        return np.exp2(np.random.permutation(np.resize(levels, k // 32))).repeat(32)
    a = np.empty((k // 512, 16))
    for p in range(k // 512):
        a[p, :8] = np.random.permutation(np.resize(levels, 8))
        for g in range(8):
            far = levels[np.abs(levels - a[p, g]) >= 10]
            a[p, g + 8] = far[np.random.randint(len(far))]
    return np.exp2(a.ravel()).repeat(32)


def f64(x):
    return np.asarray(x).astype(np.float64)


def striped(idx):
    return np.tile(np.asarray(idx).reshape(-1, 16).T, (8, 1)).astype(np.uint16)


def unstriped(offs):
    return offs[:16].T.reshape(-1).astype(np.int64)


E2M1 = np.array([0.0, 0.5, 1.0, 1.5, 2.0, 3.0, 4.0, 6.0, -0.0, -0.5, -1.0, -1.5, -2.0, -3.0, -4.0, -6.0])


def pack_weight(w, fmt):
    k, n = w.shape
    w = f64(np.asarray(w, np.float32).astype(ml_dtypes.bfloat16)).reshape(k // 32, 32, n)
    amax = np.abs(w).max(1)
    if fmt == "e4m3":
        byte = np.frexp(amax)[1] - 1 + 127 - 7
    else:
        mant, ex = np.frexp(amax / 6.0)
        byte = np.where(mant > 0.5, ex, ex - 1) + 127
    byte = np.clip(np.where(amax > 0, byte, 1), 1, 254)
    scaled = (w * np.exp2(127.0 - byte)[:, None, :]).reshape(k, n).astype(np.float32)
    by_word = np.ascontiguousarray(scaled.reshape(k // 512, 128, 4, n).transpose(0, 1, 3, 2))
    if fmt == "e4m3":
        words = by_word.astype(ml_dtypes.float8_e4m3fn).view(np.uint8)
    else:
        c = by_word.astype(ml_dtypes.float4_e2m1fn).view(np.uint8) & 0xF
        words = (c[..., 0::2] | (c[..., 1::2] << 4)).reshape(k // 512, 128, 2 * n)
    return np.ascontiguousarray(words), np.ascontiguousarray(byte.astype(np.uint8).reshape(k // 512, 16, n))


def unpack_weight(words, scales, fmt):
    g, _, n = scales.shape
    words = np.ascontiguousarray(words).reshape(g, 128, n, -1)
    if fmt == "e4m3":
        vals = words.view(ml_dtypes.float8_e4m3fn).astype(np.float64)
    else:
        nib = np.empty((g, 128, n, 4), np.uint8)
        nib[..., 0::2] = words & 0xF
        nib[..., 1::2] = words >> 4
        vals = E2M1[nib]
    vals = vals * np.repeat(np.exp2(scales.astype(np.float64) - 127.0), 8, axis=1)[..., None]
    return vals.transpose(0, 1, 3, 2).reshape(g * 512, n)


def bf(x):
    return np.asarray(x, np.float32).astype(ml_dtypes.bfloat16)


def planes(Y):
    r, m = Y.shape
    b = f64(bf(Y)).reshape(r // 32, 32, m)
    amax = np.abs(b).max(1)
    byte = np.clip(np.where(amax > 0, np.frexp(amax)[1] - 1 + 127 - 7, 1), 1, 254)
    codes = (b * np.exp2(127.0 - byte)[:, None, :]).reshape(r, m).astype(np.float32).astype(ml_dtypes.float8_e4m3fn).view(np.uint8)
    words = codes.reshape(r // 512, 128, 4, m).transpose(0, 1, 3, 2)
    return np.ascontiguousarray(words), np.ascontiguousarray(byte.astype(np.uint8).reshape(r // 512, 16, m))


K, T, J, I, N = 1024, 1024, 512, 512, 512


def setup_inputs():
    n = np.random.standard_normal
    idx = np.random.permutation(T)[:J]
    idx2 = np.random.permutation(T)[:I]
    fk = mx_kscale(K)
    fj = mx_kscale(J)
    xqp = pack_weight(n((K, T)) / fk[:, None], "e2m1")
    wap = pack_weight(n((K, N)) * 1 / np.sqrt(K) * fk[:, None], "e4m3")
    mixp = pack_weight(n((J, I)) * 1 / np.sqrt(J) * fj[:, None], "e2m1")
    return {
        "xq_words": xqp[0],
        "xq_scales": xqp[1],
        "wa_words": wap[0],
        "wa_scales": wap[1],
        "cj": (np.random.uniform(0.5, 2.0, (1, J)) / fj).astype(np.float32),
        "mix_words": mixp[0],
        "mix_scales": mixp[1],
        "res": (1.0 * n((N, T))).astype(np.float32),
        "offs": striped(idx),
        "offs2": striped(idx2),
    }


def reference(xq_words, xq_scales, wa_words, wa_scales, cj, mix_words, mix_scales, res, offs, offs2):
    idx = unstriped(offs)
    idx2 = unstriped(offs2)
    xqu = unpack_weight(xq_words, xq_scales, "e2m1")
    wau = unpack_weight(wa_words, wa_scales, "e4m3")
    mixu = unpack_weight(mix_words, mix_scales, "e2m1")
    xqidxg = xqu[:, idx]
    a = wau.T @ xqidxg
    aw = a * f64(cj)
    at = aw.T
    atq = mxq(at, 0, "e4m3")
    m = atq.T @ mixu
    mp = np.zeros((N, T))
    mp[:, idx2] = m
    y = 0.3 * f64(res) + mp
    words, scales = planes(y)
    return y, words, scales

@@ -1,0 +1,213 @@
+from contextlib import ExitStack
+
+import concourse.mybir as mybir
+
+K, T, J, I, N = 1024, 1024, 512, 512, 512
+FLOPS = 2 * K * J * N + 2 * J * I * N
+
+F32 = mybir.dt.float32
+BF16 = mybir.dt.bfloat16
+I32 = mybir.dt.int32
+U32 = mybir.dt.uint32
+U16 = mybir.dt.uint16
+U8 = mybir.dt.uint8
+FP8X4 = mybir.dt.float8_e4m3fn_x4
+FP4X4 = mybir.dt.float4_e2m1fn_x4
+MULT = mybir.AluOpType.mult
+ADD = mybir.AluOpType.add
+
+P = 128
+PACK = 4
+PASSES = K // (P * PACK)
+QUADS = 4
+CHUNKS = 4
+CW = T // CHUNKS
+
+
+def tile_list_expert_slot_mixing_pl_kernel(tc, xq_words, xq_scales, wa_words, wa_scales, cj, mix_words, mix_scales, res, offs, offs2, out_0, out_1, out_2):
+    nc = tc.nc
+    with ExitStack() as ctx:
+        keep = ctx.enter_context(tc.tile_pool(name="keep", bufs=1))
+        psum = ctx.enter_context(tc.psum_pool(name="psum", bufs=1))
+
+        def sb(shape, dtype, name, tag=None):
+            return keep.tile(shape, dtype, name=name, tag=tag or name, align_bytes=64)
+
+        pick = sb([P, J // 16], U16, "pick")
+        place = sb([P, I // 16], U16, "place")
+        x_scale = sb([P, T], U8, "x_scale")
+        w_scale = sb([P, PASSES * N], U8, "w_scale")
+        m_scale = sb([P, I], U8, "m_scale")
+        moved_scale = sb([P, J], U8, "moved_scale")
+        x_word = [sb([P, T], U16, f"x_word{z}") for z in range(PASSES)]
+        w_word = sb([P, PASSES, N], I32, "w_word")
+        m_word = sb([P, 2 * I], U8, "m_word")
+        factor = sb([P, PACK], F32, "factor")
+        page = [sb([P, T], F32, f"page{h}") for h in range(2)]
+
+        nc.vector.memset(x_scale[:].bitcast(I32), 0)
+        nc.vector.memset(w_scale[:].bitcast(I32), 0)
+        nc.vector.memset(m_scale[:].bitcast(I32), 0)
+        nc.vector.memset(moved_scale[:].bitcast(I32), 0)
+        nc.sync.dma_start(pick[:], offs)
+        for q in range(QUADS):
+            nc.sync.dma_start(
+                out=x_scale[32 * q : 32 * q + 4 * PASSES, :].bitcast(I32),
+                in_=xq_scales[:, 4 * q : 4 * q + 4, :].bitcast(I32),
+            )
+        nc.sync.dma_start(out=x_word[0][:].bitcast(I32), in_=xq_words[0].bitcast(I32))
+        nc.sync.dma_start(place[:], offs2)
+        nc.sync.dma_start(out=factor[:], in_=cj.rearrange("o (p t) -> (o p) t", t=PACK))
+        nc.sync.dma_start(out=x_word[1][:].bitcast(I32), in_=xq_words[1].bitcast(I32))
+        nc.sync.dma_start(out=w_word[:], in_=wa_words.rearrange("z p n t -> p z (n t)").bitcast(I32))
+        for q in range(QUADS):
+            nc.sync.dma_start(
+                out=w_scale[32 * q : 32 * q + 4, :].bitcast(I32).rearrange("r (z c) -> r z c", z=PASSES),
+                in_=wa_scales[:, 4 * q : 4 * q + 4, :].bitcast(I32).rearrange("z r c -> r z c"),
+            )
+        nc.sync.dma_start(out=m_word[:].bitcast(I32), in_=mix_words[0].bitcast(I32))
+        for q in range(QUADS):
+            nc.gpsimd.dma_start(
+                out=m_scale[32 * q : 32 * q + 4, :].bitcast(I32),
+                in_=mix_scales[0, 4 * q : 4 * q + 4, :].bitcast(I32),
+            )
+        res_rows = res.rearrange("(p r) t -> p r t", r=PACK)
+        out_rows = out_0.rearrange("(p r) t -> p r t", r=PACK)
+        for h in range(2):
+            nc.vector.memset(page[h][:].bitcast(I32), 0)
+
+        g_scale = sb([P, J], U8, "g_scale")
+        d_scale = sb([P, J], U8, "d_scale")
+        nc.vector.tensor_copy(g_scale[:], x_scale[:].indirect(pick[:]))
+        nc.vector.tensor_copy(
+            out=d_scale[:].rearrange("p (t q) -> p t q", t=PACK),
+            in_=g_scale[:].rearrange("p (q t) -> p t q", t=PACK),
+        )
+        for q in range(QUADS):
+            nc.scalar.dma_start(
+                out=moved_scale[32 * q : 32 * q + 4, :].bitcast(I32),
+                in_=d_scale[32 * q + 4 : 32 * q + 8, :].bitcast(I32),
+            )
+        slot_scale = [d_scale, moved_scale]
+        resid = []
+
+        def load_residual(h, tag):
+            resid.append(sb([P, 2, T], F32, f"resid{h}", tag))
+            nc.sync.dma_start(out=resid[h][:], in_=res_rows[:, 2 * h : 2 * h + 2, :])
+
+        load_residual(0, "g_scale")
+
+        bank = [psum.tile([P, PACK, P], F32, name=f"bank{b}") for b in range(PACK)]
+        for z in range(PASSES):
+            g_word = sb([P, J], U16, f"g_word{z}")
+            d_word = sb([P, J], U16, f"d_word{z}")
+            nc.vector.tensor_copy(g_word[:], x_word[z][:].indirect(pick[:]))
+            nc.vector.tensor_copy(
+                out=d_word[:].rearrange("p (t q) -> p t q", t=PACK),
+                in_=g_word[:].rearrange("p (q t) -> p t q", t=PACK),
+            )
+            if z == 0:
+                load_residual(1, "g_word0")
+            for b in range(PACK):
+                for t in range(PACK):
+                    nc.tensor.matmul_mx(
+                        out=bank[b][:, t, :],
+                        lhsT=d_word[:, P * t : P * (t + 1)].bitcast(FP4X4),
+                        lhsT_scale=slot_scale[z][:, P * t : P * (t + 1)],
+                        rhs=w_word[:, z, P * b : P * (b + 1)].bitcast(FP8X4),
+                        rhs_scale=w_scale[:, N * z + P * b : N * z + P * (b + 1)],
+                        start=(z == 0 and t == 0),
+                        stop=(z == PASSES - 1 and t == PACK - 1),
+                    )
+
+        at = sb([P, PACK, P, PACK], BF16, "at")
+        at_code = sb([P, N], U32, "at_code")
+        at_scale = sb([P, N], U8, "at_scale")
+
+        def scale_and_round(b, r0, r1):
+            nc.vector.tensor_tensor(
+                out=at[:, r0:r1, 32 * b : 32 * (b + 1), :],
+                in0=bank[b][:].rearrange("p t (q r) -> p r q t", r=PACK)[:, r0:r1],
+                in1=factor[:].unsqueeze(1).unsqueeze(1).to_broadcast([P, r1 - r0, 32, PACK]),
+                op=MULT,
+            )
+
+        def quantise_at(r0, r1):
+            nc.vector.quantize_mx(
+                out=at_code[:, P * r0 : P * r1].bitcast(FP8X4),
+                scales=at_scale[:, P * r0 : P * r1],
+                in_=at[:, r0:r1].rearrange("p r q t -> p (r q t)"),
+            )
+
+        mixed = [sb([P, I], F32, f"mixed{r}") for r in range(PACK)]
+
+        def mix(r):
+            acc = psum.tile([P, I], F32, name=f"acc{r}")
+            nc.tensor.matmul_mx(
+                out=acc[:],
+                lhsT=at_code[:, P * r : P * (r + 1)].bitcast(FP8X4),
+                lhsT_scale=at_scale[:, P * r : P * (r + 1)],
+                rhs=m_word[:].bitcast(FP4X4),
+                rhs_scale=m_scale[:],
+                start=True,
+                stop=True,
+            )
+            nc.scalar.copy(out=mixed[r][:], in_=acc[:])
+
+        for b in range(PACK - 1):
+            scale_and_round(b, 0, PACK)
+        scale_and_round(PACK - 1, 0, 1)
+        scale_and_round(PACK - 1, 1, 2)
+        quantise_at(0, 1)
+        mix(0)
+        scale_and_round(PACK - 1, 2, PACK)
+        quantise_at(1, 2)
+        mix(1)
+        quantise_at(2, PACK)
+        mix(2)
+        mix(3)
+
+        y = [sb([P, 2, T], F32, f"y{h}") for h in range(2)]
+        woven = [sb([P, CW, PACK], BF16, f"woven{c}") for c in range(CHUNKS)]
+        y_code = [sb([P, CW], I32, f"y_code{c}") for c in range(CHUNKS)]
+        y_scale = sb([P, T], U8, "y_scale")
+
+        def add_residual(r, cols):
+            nc.vector.scalar_tensor_tensor(
+                out=y[r // 2][:, r % 2, cols], in0=resid[r // 2][:, r % 2, cols], scalar=0.3, in1=page[r % 2][:, cols], op0=MULT, op1=ADD
+            )
+            nc.sync.dma_start(out=out_rows[:, r, cols], in_=y[r // 2][:, r % 2, cols])
+
+        def weave(copy, h, c):
+            copy(out=woven[c][:, :, 2 * h : 2 * h + 2], in_=y[h][:, :, CW * c : CW * (c + 1)].rearrange("p r t -> p t r"))
+
+        for r in range(PACK - 1):
+            nc.vector.tensor_copy(page[r % 2][:].indirect(place[:]), mixed[r][:])
+            scaled = sb([P, T], F32, f"scaled{r}")
+            nc.scalar.mul(out=scaled[:], in_=resid[r // 2][:, r % 2, :], mul=0.3)
+            nc.gpsimd.tensor_tensor(out=y[r // 2][:, r % 2, :], in0=scaled[:], in1=page[r % 2][:], op=ADD)
+            nc.sync.dma_start(out=out_rows[:, r, :], in_=y[r // 2][:, r % 2, :])
+            if r == 1:
+                for c in range(CHUNKS):
+                    weave(nc.scalar.copy, 0, c)
+        r = PACK - 1
+        nc.vector.tensor_copy(page[r % 2][:].indirect(place[:]), mixed[r][:])
+        for c in range(CHUNKS):
+            add_residual(r, slice(CW * c, CW * (c + 1)))
+        for c in range(CHUNKS):
+            weave(nc.scalar.copy if c < CHUNKS // 2 else nc.vector.tensor_copy, 1, c)
+        words_out = out_1[0].rearrange("p c t -> p (c t)").bitcast(I32)
+        for c in (2, 3, 0, 1):
+            cols = slice(CW * c, CW * (c + 1))
+            nc.vector.quantize_mx(
+                out=y_code[c][:].bitcast(FP8X4),
+                scales=y_scale[:, cols],
+                in_=woven[c][:].rearrange("p t r -> p (t r)"),
+            )
+            nc.sync.dma_start(out=words_out[:, cols], in_=y_code[c][:])
+        for q in range(QUADS):
+            eng = nc.scalar if q % 2 else nc.sync
+            eng.dma_start(
+                out=out_2[0, 4 * q : 4 * q + 4, :].bitcast(I32),
+                in_=y_scale[32 * q : 32 * q + 4, :].bitcast(I32),
+            )

@@ -40,12 +40,12 @@ def tile_list_expert_slot_mixing_pl_kernel(tc, xq_words, xq_scales, wa_words, wa
         m_scale = sb([P, I], U8, "m_scale")
         moved_scale = sb([P, J], U8, "moved_scale")
         x_word = [sb([P, T], U16, f"x_word{z}") for z in range(PASSES)]
-        w_word = sb([P, PASSES, N], I32, "w_word")
-        m_word = sb([P, 2 * I], U8, "m_word")
+        w_word = [sb([P, N], I32, f"w_word{z}") for z in range(PASSES)]
         factor = sb([P, PACK], F32, "factor")
         page = [sb([P, T], F32, f"page{h}") for h in range(2)]
 
         nc.vector.memset(x_scale[:].bitcast(I32), 0)
+        nc.vector.memset(page[0][:].bitcast(I32), 0)
         nc.vector.memset(w_scale[:].bitcast(I32), 0)
         nc.vector.memset(m_scale[:].bitcast(I32), 0)
         nc.vector.memset(moved_scale[:].bitcast(I32), 0)
@@ -56,29 +56,39 @@ def tile_list_expert_slot_mixing_pl_kernel(tc, xq_words, xq_scales, wa_words, wa
                 in_=xq_scales[:, 4 * q : 4 * q + 4, :].bitcast(I32),
             )
         nc.sync.dma_start(out=x_word[0][:].bitcast(I32), in_=xq_words[0].bitcast(I32))
-        nc.sync.dma_start(place[:], offs2)
-        nc.sync.dma_start(out=factor[:], in_=cj.rearrange("o (p t) -> (o p) t", t=PACK))
-        nc.sync.dma_start(out=x_word[1][:].bitcast(I32), in_=xq_words[1].bitcast(I32))
-        nc.sync.dma_start(out=w_word[:], in_=wa_words.rearrange("z p n t -> p z (n t)").bitcast(I32))
+        nc.gpsimd.dma_start(out=x_word[1][:].bitcast(I32), in_=xq_words[1].bitcast(I32))
+        nc.sync.dma_start(out=w_word[0][:], in_=wa_words[0].rearrange("p n t -> p (n t)").bitcast(I32))
         for q in range(QUADS):
-            nc.sync.dma_start(
+            nc.scalar.dma_start(
                 out=w_scale[32 * q : 32 * q + 4, :].bitcast(I32).rearrange("r (z c) -> r z c", z=PASSES),
                 in_=wa_scales[:, 4 * q : 4 * q + 4, :].bitcast(I32).rearrange("z r c -> r z c"),
             )
-        nc.sync.dma_start(out=m_word[:].bitcast(I32), in_=mix_words[0].bitcast(I32))
+        nc.sync.dma_start(place[:], offs2)
+        nc.gpsimd.dma_start(out=w_word[1][:], in_=wa_words[1].rearrange("p n t -> p (n t)").bitcast(I32))
+        nc.gpsimd.dma_start(out=factor[:], in_=cj.rearrange("o (p t) -> (o p) t", t=PACK))
         for q in range(QUADS):
-            nc.gpsimd.dma_start(
+            nc.scalar.dma_start(
                 out=m_scale[32 * q : 32 * q + 4, :].bitcast(I32),
                 in_=mix_scales[0, 4 * q : 4 * q + 4, :].bitcast(I32),
             )
         res_rows = res.rearrange("(p r) t -> p r t", r=PACK)
         out_rows = out_0.rearrange("(p r) t -> p r t", r=PACK)
-        for h in range(2):
-            nc.vector.memset(page[h][:].bitcast(I32), 0)
+        nc.vector.memset(page[1][:].bitcast(I32), 0)
 
         g_scale = sb([P, J], U8, "g_scale")
         d_scale = sb([P, J], U8, "d_scale")
         nc.vector.tensor_copy(g_scale[:], x_scale[:].indirect(pick[:]))
+        warm = psum.tile([P, I], F32, name="warm", tag="acc3")
+        for i in range(3):
+            nc.tensor.matmul_mx(
+                out=warm[:],
+                lhsT=w_word[0][:, 0:P].bitcast(FP8X4),
+                lhsT_scale=w_scale[:, 0:P],
+                rhs=x_word[1][:, 0:J].bitcast(FP4X4),
+                rhs_scale=g_scale[:],
+                start=True,
+                stop=True,
+            )
         nc.vector.tensor_copy(
             out=d_scale[:].rearrange("p (t q) -> p t q", t=PACK),
             in_=g_scale[:].rearrange("p (q t) -> p t q", t=PACK),
@@ -95,33 +105,34 @@ def tile_list_expert_slot_mixing_pl_kernel(tc, xq_words, xq_scales, wa_words, wa
             resid.append(sb([P, 2, T], F32, f"resid{h}", tag))
             nc.sync.dma_start(out=resid[h][:], in_=res_rows[:, 2 * h : 2 * h + 2, :])
 
-        load_residual(0, "g_scale")
+        m_word = sb([P, 2 * I], U8, "m_word", "g_scale")
+        nc.sync.dma_start(out=m_word[:].bitcast(I32), in_=mix_words[0].bitcast(I32))
 
         bank = [psum.tile([P, PACK, P], F32, name=f"bank{b}") for b in range(PACK)]
         for z in range(PASSES):
-            g_word = sb([P, J], U16, f"g_word{z}")
+            g_tag = ("x_scale", "x_word0")[z]
+            g_word = sb([P, J], U16, f"g_word{z}", g_tag)
             d_word = sb([P, J], U16, f"d_word{z}")
             nc.vector.tensor_copy(g_word[:], x_word[z][:].indirect(pick[:]))
             nc.vector.tensor_copy(
                 out=d_word[:].rearrange("p (t q) -> p t q", t=PACK),
                 in_=g_word[:].rearrange("p (q t) -> p t q", t=PACK),
             )
-            if z == 0:
-                load_residual(1, "g_word0")
+            load_residual(z, g_tag)
             for b in range(PACK):
                 for t in range(PACK):
                     nc.tensor.matmul_mx(
                         out=bank[b][:, t, :],
                         lhsT=d_word[:, P * t : P * (t + 1)].bitcast(FP4X4),
                         lhsT_scale=slot_scale[z][:, P * t : P * (t + 1)],
-                        rhs=w_word[:, z, P * b : P * (b + 1)].bitcast(FP8X4),
+                        rhs=w_word[z][:, P * b : P * (b + 1)].bitcast(FP8X4),
                         rhs_scale=w_scale[:, N * z + P * b : N * z + P * (b + 1)],
                         start=(z == 0 and t == 0),
                         stop=(z == PASSES - 1 and t == PACK - 1),
                     )
 
         at = sb([P, PACK, P, PACK], BF16, "at")
-        at_code = sb([P, N], U32, "at_code")
+        at_code = [sb([P, P], U32, f"at_code{r}") for r in range(PACK)]
         at_scale = sb([P, N], U8, "at_scale")
 
         def scale_and_round(b, r0, r1):
@@ -132,20 +143,20 @@ def tile_list_expert_slot_mixing_pl_kernel(tc, xq_words, xq_scales, wa_words, wa
                 op=MULT,
             )
 
-        def quantise_at(r0, r1):
+        def quantise_at(r):
             nc.vector.quantize_mx(
-                out=at_code[:, P * r0 : P * r1].bitcast(FP8X4),
-                scales=at_scale[:, P * r0 : P * r1],
-                in_=at[:, r0:r1].rearrange("p r q t -> p (r q t)"),
+                out=at_code[r][:].bitcast(FP8X4),
+                scales=at_scale[:, P * r : P * (r + 1)],
+                in_=at[:, r].rearrange("p q t -> p (q t)"),
             )
 
         mixed = [sb([P, I], F32, f"mixed{r}") for r in range(PACK)]
 
         def mix(r):
-            acc = psum.tile([P, I], F32, name=f"acc{r}")
+            acc = psum.tile([P, I], F32, name=f"acc{r}", tag=f"acc{r}")
             nc.tensor.matmul_mx(
                 out=acc[:],
-                lhsT=at_code[:, P * r : P * (r + 1)].bitcast(FP8X4),
+                lhsT=at_code[r][:].bitcast(FP8X4),
                 lhsT_scale=at_scale[:, P * r : P * (r + 1)],
                 rhs=m_word[:].bitcast(FP4X4),
                 rhs_scale=m_scale[:],
@@ -155,17 +166,18 @@ def tile_list_expert_slot_mixing_pl_kernel(tc, xq_words, xq_scales, wa_words, wa
             nc.scalar.copy(out=mixed[r][:], in_=acc[:])
 
         for b in range(PACK - 1):
-            scale_and_round(b, 0, PACK)
+            scale_and_round(b, 0, 2)
         scale_and_round(PACK - 1, 0, 1)
         scale_and_round(PACK - 1, 1, 2)
-        quantise_at(0, 1)
+        quantise_at(0)
         mix(0)
-        scale_and_round(PACK - 1, 2, PACK)
-        quantise_at(1, 2)
+        quantise_at(1)
         mix(1)
-        quantise_at(2, PACK)
-        mix(2)
-        mix(3)
+        for b in range(PACK):
+            scale_and_round(b, 2, PACK)
+        for r in range(2, PACK):
+            quantise_at(r)
+            mix(r)
 
         y = [sb([P, 2, T], F32, f"y{h}") for h in range(2)]
         woven = [sb([P, CW, PACK], BF16, f"woven{c}") for c in range(CHUNKS)]
@@ -183,7 +195,7 @@ def tile_list_expert_slot_mixing_pl_kernel(tc, xq_words, xq_scales, wa_words, wa
 
         for r in range(PACK - 1):
             nc.vector.tensor_copy(page[r % 2][:].indirect(place[:]), mixed[r][:])
-            scaled = sb([P, T], F32, f"scaled{r}")
+            scaled = sb([P, T], F32, f"scaled{r}", f"at_code{r}")
             nc.scalar.mul(out=scaled[:], in_=resid[r // 2][:, r % 2, :], mul=0.3)
             nc.gpsimd.tensor_tensor(out=y[r // 2][:, r % 2, :], in0=scaled[:], in1=page[r % 2][:], op=ADD)
             nc.sync.dma_start(out=out_rows[:, r, :], in_=y[r // 2][:, r % 2, :])

@@ -42,7 +42,7 @@ def tile_list_expert_slot_mixing_pl_kernel(tc, xq_words, xq_scales, wa_words, wa
         x_word = [sb([P, T], U16, f"x_word{z}") for z in range(PASSES)]
         w_word = [sb([P, N], I32, f"w_word{z}") for z in range(PASSES)]
         factor = sb([P, PACK], F32, "factor")
-        page = [sb([P, T], F32, f"page{h}") for h in range(2)]
+        page = [sb([P, T], F32, "page0")]
 
         nc.vector.memset(x_scale[:].bitcast(I32), 0)
         nc.vector.memset(page[0][:].bitcast(I32), 0)
@@ -50,16 +50,16 @@ def tile_list_expert_slot_mixing_pl_kernel(tc, xq_words, xq_scales, wa_words, wa
         nc.vector.memset(m_scale[:].bitcast(I32), 0)
         nc.vector.memset(moved_scale[:].bitcast(I32), 0)
         nc.sync.dma_start(pick[:], offs)
+        nc.sync.dma_start(out=x_word[0][:].bitcast(I32), in_=xq_words[0].bitcast(I32))
         for q in range(QUADS):
             nc.sync.dma_start(
                 out=x_scale[32 * q : 32 * q + 4 * PASSES, :].bitcast(I32),
                 in_=xq_scales[:, 4 * q : 4 * q + 4, :].bitcast(I32),
             )
-        nc.sync.dma_start(out=x_word[0][:].bitcast(I32), in_=xq_words[0].bitcast(I32))
         nc.gpsimd.dma_start(out=x_word[1][:].bitcast(I32), in_=xq_words[1].bitcast(I32))
         nc.sync.dma_start(out=w_word[0][:], in_=wa_words[0].rearrange("p n t -> p (n t)").bitcast(I32))
         for q in range(QUADS):
-            nc.scalar.dma_start(
+            nc.sync.dma_start(
                 out=w_scale[32 * q : 32 * q + 4, :].bitcast(I32).rearrange("r (z c) -> r z c", z=PASSES),
                 in_=wa_scales[:, 4 * q : 4 * q + 4, :].bitcast(I32).rearrange("z r c -> r z c"),
             )
@@ -67,69 +67,76 @@ def tile_list_expert_slot_mixing_pl_kernel(tc, xq_words, xq_scales, wa_words, wa
         nc.gpsimd.dma_start(out=w_word[1][:], in_=wa_words[1].rearrange("p n t -> p (n t)").bitcast(I32))
         nc.gpsimd.dma_start(out=factor[:], in_=cj.rearrange("o (p t) -> (o p) t", t=PACK))
         for q in range(QUADS):
-            nc.scalar.dma_start(
+            nc.sync.dma_start(
                 out=m_scale[32 * q : 32 * q + 4, :].bitcast(I32),
                 in_=mix_scales[0, 4 * q : 4 * q + 4, :].bitcast(I32),
             )
         res_rows = res.rearrange("(p r) t -> p r t", r=PACK)
         out_rows = out_0.rearrange("(p r) t -> p r t", r=PACK)
-        nc.vector.memset(page[1][:].bitcast(I32), 0)
 
-        g_scale = sb([P, J], U8, "g_scale")
-        d_scale = sb([P, J], U8, "d_scale")
+        g_word0 = sb([P, J], U16, "g_word0")
+        nc.vector.tensor_copy(g_word0[:], x_word[0][:].indirect(pick[:]))
+        g_scale = sb([P, J], U8, "g_scale", "x_word0")
         nc.vector.tensor_copy(g_scale[:], x_scale[:].indirect(pick[:]))
         warm = psum.tile([P, I], F32, name="warm", tag="acc3")
         for i in range(3):
             nc.tensor.matmul_mx(
                 out=warm[:],
                 lhsT=w_word[0][:, 0:P].bitcast(FP8X4),
-                lhsT_scale=w_scale[:, 0:P],
-                rhs=x_word[1][:, 0:J].bitcast(FP4X4),
-                rhs_scale=g_scale[:],
+                lhsT_scale=x_scale[:, 0:P],
+                rhs=g_word0[:].bitcast(FP4X4),
+                rhs_scale=x_scale[:, 0:J],
                 start=True,
                 stop=True,
             )
-        nc.vector.tensor_copy(
-            out=d_scale[:].rearrange("p (t q) -> p t q", t=PACK),
-            in_=g_scale[:].rearrange("p (q t) -> p t q", t=PACK),
-        )
-        for q in range(QUADS):
-            nc.scalar.dma_start(
-                out=moved_scale[32 * q : 32 * q + 4, :].bitcast(I32),
-                in_=d_scale[32 * q + 4 : 32 * q + 8, :].bitcast(I32),
+
+        def deal(src, dtype, name):
+            dealt = sb([P, J], dtype, name)
+            nc.vector.tensor_copy(
+                out=dealt[:].rearrange("p (t q) -> p t q", t=PACK),
+                in_=src[:].rearrange("p (q t) -> p t q", t=PACK),
             )
-        slot_scale = [d_scale, moved_scale]
+            return dealt
+
+        bank = [psum.tile([P, PACK, P], F32, name=f"bank{b}") for b in range(PACK)]
+
+        def expert_pass(z, words, scales):
+            for b in range(PACK):
+                for t in range(PACK):
+                    nc.tensor.matmul_mx(
+                        out=bank[b][:, t, :],
+                        lhsT=words[:, P * t : P * (t + 1)].bitcast(FP4X4),
+                        lhsT_scale=scales[:, P * t : P * (t + 1)],
+                        rhs=w_word[z][:, P * b : P * (b + 1)].bitcast(FP8X4),
+                        rhs_scale=w_scale[:, N * z + P * b : N * z + P * (b + 1)],
+                        start=(z == 0 and t == 0),
+                        stop=(z == PASSES - 1 and t == PACK - 1),
+                    )
+
         resid = []
 
         def load_residual(h, tag):
             resid.append(sb([P, 2, T], F32, f"resid{h}", tag))
             nc.sync.dma_start(out=resid[h][:], in_=res_rows[:, 2 * h : 2 * h + 2, :])
 
-        m_word = sb([P, 2 * I], U8, "m_word", "g_scale")
-        nc.sync.dma_start(out=m_word[:].bitcast(I32), in_=mix_words[0].bitcast(I32))
-
-        bank = [psum.tile([P, PACK, P], F32, name=f"bank{b}") for b in range(PACK)]
-        for z in range(PASSES):
-            g_tag = ("x_scale", "x_word0")[z]
-            g_word = sb([P, J], U16, f"g_word{z}", g_tag)
-            d_word = sb([P, J], U16, f"d_word{z}")
-            nc.vector.tensor_copy(g_word[:], x_word[z][:].indirect(pick[:]))
-            nc.vector.tensor_copy(
-                out=d_word[:].rearrange("p (t q) -> p t q", t=PACK),
-                in_=g_word[:].rearrange("p (q t) -> p t q", t=PACK),
+        d_word0 = deal(g_word0, U16, "d_word0")
+        d_scale = deal(g_scale, U8, "d_scale")
+        for q in range(QUADS):
+            (nc.sync if q % 2 else nc.scalar).dma_start(
+                out=moved_scale[32 * q : 32 * q + 4, :].bitcast(I32),
+                in_=d_scale[32 * q + 4 : 32 * q + 8, :].bitcast(I32),
             )
-            load_residual(z, g_tag)
-            for b in range(PACK):
-                for t in range(PACK):
-                    nc.tensor.matmul_mx(
-                        out=bank[b][:, t, :],
-                        lhsT=d_word[:, P * t : P * (t + 1)].bitcast(FP4X4),
-                        lhsT_scale=slot_scale[z][:, P * t : P * (t + 1)],
-                        rhs=w_word[z][:, P * b : P * (b + 1)].bitcast(FP8X4),
-                        rhs_scale=w_scale[:, N * z + P * b : N * z + P * (b + 1)],
-                        start=(z == 0 and t == 0),
-                        stop=(z == PASSES - 1 and t == PACK - 1),
-                    )
+        m_word = sb([P, 2 * I], U8, "m_word", "x_word0")
+        nc.sync.dma_start(out=m_word[:].bitcast(I32), in_=mix_words[0].bitcast(I32))
+        expert_pass(0, d_word0, d_scale)
+        g_word1 = sb([P, J], U16, "g_word1", "x_scale")
+        nc.vector.tensor_copy(g_word1[:], x_word[1][:].indirect(pick[:]))
+        d_word1 = deal(g_word1, U16, "d_word1")
+        load_residual(0, "x_word1")
+        load_residual(1, "d_word0")
+        page.append(sb([P, T], F32, "page1", "x_scale"))
+        nc.vector.memset(page[1][:].bitcast(I32), 0)
+        expert_pass(1, d_word1, moved_scale)
 
         at = sb([P, PACK, P, PACK], BF16, "at")
         at_code = [sb([P, P], U32, f"at_code{r}") for r in range(PACK)]
@@ -142,6 +149,15 @@ def tile_list_expert_slot_mixing_pl_kernel(tc, xq_words, xq_scales, wa_words, wa
                 in1=factor[:].unsqueeze(1).unsqueeze(1).to_broadcast([P, r1 - r0, 32, PACK]),
                 op=MULT,
             )
+
+        def scale_and_round_on_scalar(b, r0, r1):
+            for t in range(PACK):
+                nc.scalar.activation(
+                    out=at[:, r0:r1, 32 * b : 32 * (b + 1), t],
+                    in_=bank[b][:, t, :].rearrange("p (q r) -> p r q", r=PACK)[:, r0:r1],
+                    func=mybir.ActivationFunctionType.Copy,
+                    scale=factor[:, t : t + 1],
+                )
 
         def quantise_at(r):
             nc.vector.quantize_mx(
@@ -167,13 +183,15 @@ def tile_list_expert_slot_mixing_pl_kernel(tc, xq_words, xq_scales, wa_words, wa
 
         for b in range(PACK - 1):
             scale_and_round(b, 0, 2)
+            if b < 2:
+                scale_and_round_on_scalar(b, 2, PACK)
         scale_and_round(PACK - 1, 0, 1)
         scale_and_round(PACK - 1, 1, 2)
         quantise_at(0)
         mix(0)
         quantise_at(1)
         mix(1)
-        for b in range(PACK):
+        for b in range(2, PACK):
             scale_and_round(b, 2, PACK)
         for r in range(2, PACK):
             quantise_at(r)
@@ -181,14 +199,13 @@ def tile_list_expert_slot_mixing_pl_kernel(tc, xq_words, xq_scales, wa_words, wa
 
         y = [sb([P, 2, T], F32, f"y{h}") for h in range(2)]
         woven = [sb([P, CW, PACK], BF16, f"woven{c}") for c in range(CHUNKS)]
-        y_code = [sb([P, CW], I32, f"y_code{c}") for c in range(CHUNKS)]
+        y_code = sb([P, T], I32, "y_code")
         y_scale = sb([P, T], U8, "y_scale")
 
         def add_residual(r, cols):
             nc.vector.scalar_tensor_tensor(
                 out=y[r // 2][:, r % 2, cols], in0=resid[r // 2][:, r % 2, cols], scalar=0.3, in1=page[r % 2][:, cols], op0=MULT, op1=ADD
             )
-            nc.sync.dma_start(out=out_rows[:, r, cols], in_=y[r // 2][:, r % 2, cols])
 
         def weave(copy, h, c):
             copy(out=woven[c][:, :, 2 * h : 2 * h + 2], in_=y[h][:, :, CW * c : CW * (c + 1)].rearrange("p r t -> p t r"))
@@ -206,17 +223,22 @@ def tile_list_expert_slot_mixing_pl_kernel(tc, xq_words, xq_scales, wa_words, wa
         nc.vector.tensor_copy(page[r % 2][:].indirect(place[:]), mixed[r][:])
         for c in range(CHUNKS):
             add_residual(r, slice(CW * c, CW * (c + 1)))
+            if c % 2:
+                cols = slice(CW * (c - 1), CW * (c + 1))
+                nc.sync.dma_start(out=out_rows[:, r, cols], in_=y[1][:, 1, cols])
         for c in range(CHUNKS):
-            weave(nc.scalar.copy if c < CHUNKS // 2 else nc.vector.tensor_copy, 1, c)
+            weave(nc.scalar.copy if c < CHUNKS - 1 else nc.vector.tensor_copy, 1, c)
         words_out = out_1[0].rearrange("p c t -> p (c t)").bitcast(I32)
-        for c in (2, 3, 0, 1):
+        for c in (0, 3, 1, 2):
             cols = slice(CW * c, CW * (c + 1))
             nc.vector.quantize_mx(
-                out=y_code[c][:].bitcast(FP8X4),
+                out=y_code[:, cols].bitcast(FP8X4),
                 scales=y_scale[:, cols],
                 in_=woven[c][:].rearrange("p t r -> p (t r)"),
             )
-            nc.sync.dma_start(out=words_out[:, cols], in_=y_code[c][:])
+            if c != 0:
+                cols = slice(0, 2 * CW) if c == 1 else cols
+                nc.sync.dma_start(out=words_out[:, cols], in_=y_code[:, cols])
         for q in range(QUADS):
             eng = nc.scalar if q % 2 else nc.sync
             eng.dma_start(

from contextlib import ExitStack

import concourse.mybir as mybir

K, T, J, I, N = 1024, 1024, 512, 512, 512
FLOPS = 2 * K * J * N + 2 * J * I * N

F32 = mybir.dt.float32
BF16 = mybir.dt.bfloat16
I32 = mybir.dt.int32
U32 = mybir.dt.uint32
U16 = mybir.dt.uint16
U8 = mybir.dt.uint8
FP8X4 = mybir.dt.float8_e4m3fn_x4
FP4X4 = mybir.dt.float4_e2m1fn_x4
MULT = mybir.AluOpType.mult
ADD = mybir.AluOpType.add

P = 128
PACK = 4
PASSES = K // (P * PACK)
QUADS = 4
CHUNKS = 4
CW = T // CHUNKS


def tile_list_expert_slot_mixing_pl_kernel(tc, xq_words, xq_scales, wa_words, wa_scales, cj, mix_words, mix_scales, res, offs, offs2, out_0, out_1, out_2):
    nc = tc.nc
    with ExitStack() as ctx:
        keep = ctx.enter_context(tc.tile_pool(name="keep", bufs=1))
        psum = ctx.enter_context(tc.psum_pool(name="psum", bufs=1))

        def sb(shape, dtype, name, tag=None):
            return keep.tile(shape, dtype, name=name, tag=tag or name, align_bytes=64)

        pick = sb([P, J // 16], U16, "pick")
        place = sb([P, I // 16], U16, "place")
        x_scale = sb([P, T], U8, "x_scale")
        w_scale = sb([P, PASSES * N], U8, "w_scale")
        m_scale = sb([P, I], U8, "m_scale")
        moved_scale = sb([P, J], U8, "moved_scale")
        x_word = [sb([P, T], U16, f"x_word{z}") for z in range(PASSES)]
        w_word = [sb([P, N], I32, f"w_word{z}") for z in range(PASSES)]
        factor = sb([P, PACK], F32, "factor")
        page = [sb([P, T], F32, "page0")]

        nc.vector.memset(x_scale[:].bitcast(I32), 0)
        nc.vector.memset(page[0][:].bitcast(I32), 0)
        nc.vector.memset(w_scale[:].bitcast(I32), 0)
        nc.vector.memset(m_scale[:].bitcast(I32), 0)
        nc.vector.memset(moved_scale[:].bitcast(I32), 0)
        nc.sync.dma_start(pick[:], offs)
        nc.sync.dma_start(out=x_word[0][:].bitcast(I32), in_=xq_words[0].bitcast(I32))
        for q in range(QUADS):
            nc.sync.dma_start(
                out=x_scale[32 * q : 32 * q + 4 * PASSES, :].bitcast(I32),
                in_=xq_scales[:, 4 * q : 4 * q + 4, :].bitcast(I32),
            )
        nc.gpsimd.dma_start(out=x_word[1][:].bitcast(I32), in_=xq_words[1].bitcast(I32))
        nc.sync.dma_start(out=w_word[0][:], in_=wa_words[0].rearrange("p n t -> p (n t)").bitcast(I32))
        for q in range(QUADS):
            nc.sync.dma_start(
                out=w_scale[32 * q : 32 * q + 4, :].bitcast(I32).rearrange("r (z c) -> r z c", z=PASSES),
                in_=wa_scales[:, 4 * q : 4 * q + 4, :].bitcast(I32).rearrange("z r c -> r z c"),
            )
        nc.sync.dma_start(place[:], offs2)
        nc.gpsimd.dma_start(out=w_word[1][:], in_=wa_words[1].rearrange("p n t -> p (n t)").bitcast(I32))
        nc.gpsimd.dma_start(out=factor[:], in_=cj.rearrange("o (p t) -> (o p) t", t=PACK))
        for q in range(QUADS):
            nc.sync.dma_start(
                out=m_scale[32 * q : 32 * q + 4, :].bitcast(I32),
                in_=mix_scales[0, 4 * q : 4 * q + 4, :].bitcast(I32),
            )
        res_rows = res.rearrange("(p r) t -> p r t", r=PACK)
        out_rows = out_0.rearrange("(p r) t -> p r t", r=PACK)

        g_word0 = sb([P, J], U16, "g_word0")
        nc.vector.tensor_copy(g_word0[:], x_word[0][:].indirect(pick[:]))
        g_scale = sb([P, J], U8, "g_scale", "x_word0")
        nc.vector.tensor_copy(g_scale[:], x_scale[:].indirect(pick[:]))
        warm = psum.tile([P, I], F32, name="warm", tag="acc3")
        for i in range(3):
            nc.tensor.matmul_mx(
                out=warm[:],
                lhsT=w_word[0][:, 0:P].bitcast(FP8X4),
                lhsT_scale=x_scale[:, 0:P],
                rhs=g_word0[:].bitcast(FP4X4),
                rhs_scale=x_scale[:, 0:J],
                start=True,
                stop=True,
            )

        def deal(src, dtype, name):
            dealt = sb([P, J], dtype, name)
            nc.vector.tensor_copy(
                out=dealt[:].rearrange("p (t q) -> p t q", t=PACK),
                in_=src[:].rearrange("p (q t) -> p t q", t=PACK),
            )
            return dealt

        bank = [psum.tile([P, PACK, P], F32, name=f"bank{b}") for b in range(PACK)]

        def expert_pass(z, words, scales):
            for b in range(PACK):
                for t in range(PACK):
                    nc.tensor.matmul_mx(
                        out=bank[b][:, t, :],
                        lhsT=words[:, P * t : P * (t + 1)].bitcast(FP4X4),
                        lhsT_scale=scales[:, P * t : P * (t + 1)],
                        rhs=w_word[z][:, P * b : P * (b + 1)].bitcast(FP8X4),
                        rhs_scale=w_scale[:, N * z + P * b : N * z + P * (b + 1)],
                        start=(z == 0 and t == 0),
                        stop=(z == PASSES - 1 and t == PACK - 1),
                    )

        resid = []

        def load_residual(h, tag):
            resid.append(sb([P, 2, T], F32, f"resid{h}", tag))
            nc.sync.dma_start(out=resid[h][:], in_=res_rows[:, 2 * h : 2 * h + 2, :])

        d_word0 = deal(g_word0, U16, "d_word0")
        d_scale = deal(g_scale, U8, "d_scale")
        for q in range(QUADS):
            (nc.sync if q % 2 else nc.scalar).dma_start(
                out=moved_scale[32 * q : 32 * q + 4, :].bitcast(I32),
                in_=d_scale[32 * q + 4 : 32 * q + 8, :].bitcast(I32),
            )
        m_word = sb([P, 2 * I], U8, "m_word", "x_word0")
        nc.sync.dma_start(out=m_word[:].bitcast(I32), in_=mix_words[0].bitcast(I32))
        expert_pass(0, d_word0, d_scale)
        g_word1 = sb([P, J], U16, "g_word1", "x_scale")
        nc.vector.tensor_copy(g_word1[:], x_word[1][:].indirect(pick[:]))
        d_word1 = deal(g_word1, U16, "d_word1")
        load_residual(0, "x_word1")
        load_residual(1, "d_word0")
        page.append(sb([P, T], F32, "page1", "x_scale"))
        nc.vector.memset(page[1][:].bitcast(I32), 0)
        expert_pass(1, d_word1, moved_scale)

        at = sb([P, PACK, P, PACK], BF16, "at")
        at_code = [sb([P, P], U32, f"at_code{r}") for r in range(PACK)]
        at_scale = sb([P, N], U8, "at_scale")

        def scale_and_round(b, r0, r1):
            nc.vector.tensor_tensor(
                out=at[:, r0:r1, 32 * b : 32 * (b + 1), :],
                in0=bank[b][:].rearrange("p t (q r) -> p r q t", r=PACK)[:, r0:r1],
                in1=factor[:].unsqueeze(1).unsqueeze(1).to_broadcast([P, r1 - r0, 32, PACK]),
                op=MULT,
            )

        def scale_and_round_on_scalar(b, r0, r1):
            for t in range(PACK):
                nc.scalar.activation(
                    out=at[:, r0:r1, 32 * b : 32 * (b + 1), t],
                    in_=bank[b][:, t, :].rearrange("p (q r) -> p r q", r=PACK)[:, r0:r1],
                    func=mybir.ActivationFunctionType.Copy,
                    scale=factor[:, t : t + 1],
                )

        def quantise_at(r):
            nc.vector.quantize_mx(
                out=at_code[r][:].bitcast(FP8X4),
                scales=at_scale[:, P * r : P * (r + 1)],
                in_=at[:, r].rearrange("p q t -> p (q t)"),
            )

        mixed = [sb([P, I], F32, f"mixed{r}") for r in range(PACK)]

        def mix(r):
            acc = psum.tile([P, I], F32, name=f"acc{r}", tag=f"acc{r}")
            nc.tensor.matmul_mx(
                out=acc[:],
                lhsT=at_code[r][:].bitcast(FP8X4),
                lhsT_scale=at_scale[:, P * r : P * (r + 1)],
                rhs=m_word[:].bitcast(FP4X4),
                rhs_scale=m_scale[:],
                start=True,
                stop=True,
            )
            nc.scalar.copy(out=mixed[r][:], in_=acc[:])

        for b in range(PACK - 1):
            scale_and_round(b, 0, 2)
            if b < 2:
                scale_and_round_on_scalar(b, 2, PACK)
        scale_and_round(PACK - 1, 0, 1)
        scale_and_round(PACK - 1, 1, 2)
        quantise_at(0)
        mix(0)
        quantise_at(1)
        mix(1)
        for b in range(2, PACK):
            scale_and_round(b, 2, PACK)
        for r in range(2, PACK):
            quantise_at(r)
            mix(r)

        y = [sb([P, 2, T], F32, f"y{h}") for h in range(2)]
        woven = [sb([P, CW, PACK], BF16, f"woven{c}") for c in range(CHUNKS)]
        y_code = sb([P, T], I32, "y_code")
        y_scale = sb([P, T], U8, "y_scale")

        def add_residual(r, cols):
            nc.vector.scalar_tensor_tensor(
                out=y[r // 2][:, r % 2, cols], in0=resid[r // 2][:, r % 2, cols], scalar=0.3, in1=page[r % 2][:, cols], op0=MULT, op1=ADD
            )

        def weave(copy, h, c):
            copy(out=woven[c][:, :, 2 * h : 2 * h + 2], in_=y[h][:, :, CW * c : CW * (c + 1)].rearrange("p r t -> p t r"))

        for r in range(PACK - 1):
            nc.vector.tensor_copy(page[r % 2][:].indirect(place[:]), mixed[r][:])
            scaled = sb([P, T], F32, f"scaled{r}", f"at_code{r}")
            nc.scalar.mul(out=scaled[:], in_=resid[r // 2][:, r % 2, :], mul=0.3)
            nc.gpsimd.tensor_tensor(out=y[r // 2][:, r % 2, :], in0=scaled[:], in1=page[r % 2][:], op=ADD)
            nc.sync.dma_start(out=out_rows[:, r, :], in_=y[r // 2][:, r % 2, :])
            if r == 1:
                for c in range(CHUNKS):
                    weave(nc.scalar.copy, 0, c)
        r = PACK - 1
        nc.vector.tensor_copy(page[r % 2][:].indirect(place[:]), mixed[r][:])
        for c in range(CHUNKS):
            add_residual(r, slice(CW * c, CW * (c + 1)))
            if c % 2:
                cols = slice(CW * (c - 1), CW * (c + 1))
                nc.sync.dma_start(out=out_rows[:, r, cols], in_=y[1][:, 1, cols])
        for c in range(CHUNKS):
            weave(nc.scalar.copy if c < CHUNKS - 1 else nc.vector.tensor_copy, 1, c)
        words_out = out_1[0].rearrange("p c t -> p (c t)").bitcast(I32)
        for c in (0, 3, 1, 2):
            cols = slice(CW * c, CW * (c + 1))
            nc.vector.quantize_mx(
                out=y_code[:, cols].bitcast(FP8X4),
                scales=y_scale[:, cols],
                in_=woven[c][:].rearrange("p t r -> p (t r)"),
            )
            if c != 0:
                cols = slice(0, 2 * CW) if c == 1 else cols
                nc.sync.dma_start(out=words_out[:, cols], in_=y_code[:, cols])
        for q in range(QUADS):
            eng = nc.scalar if q % 2 else nc.sync
            eng.dma_start(
                out=out_2[0, 4 * q : 4 * q + 4, :].bitcast(I32),
                in_=y_scale[32 * q : 32 * q + 4, :].bitcast(I32),
            )
